import numpy as np
import ml_dtypes

BF16 = ml_dtypes.bfloat16


def bf(x):
    return np.asarray(x, np.float32).astype(BF16)


def f32(x):
    return np.asarray(x, np.float32)


def f64(x):
    return np.asarray(x).astype(np.float64)


def striped(idx):
    return np.tile(idx.reshape(-1, 16).T, (8, 1))


S, K, N, E, Q, H, O = 512, 128, 512, 2, 256, 128, 128


def gelu_tanh(v):
    return 0.5 * v * (1.0 + np.tanh(np.sqrt(2.0 / np.pi) * (v + 0.044715 * v**3)))


def setup_inputs():
    return {"table": bf(np.random.standard_normal((K, S))), "w": bf(np.random.standard_normal((E, K, H)) / np.sqrt(K)), "b": f32(0.5 * np.random.standard_normal((H, E))), "w2": bf(np.random.standard_normal((E, H, O)) / np.sqrt(H)), "offs": striped(np.sort(np.random.permutation(S).reshape(E, Q), axis=1).reshape(-1))}


def reference(table, w, b, w2, offs):
    idx = offs[:16].T.reshape(-1)
    x = f64(table)[:, idx]
    ys = []
    for e in range(E):
        t = f64(w)[e].T @ x[:, e * Q : (e + 1) * Q] + f64(b)[:, e : e + 1]
        t = gelu_tanh(t)
        ys.append(f64(w2)[e].T @ t)
    return np.concatenate(ys, axis=1)

import concourse.mybir as mybir

BF16, F32, U16 = mybir.dt.bfloat16, mybir.dt.float32, mybir.dt.uint16
GELU_TANH = mybir.ActivationFunctionType.Gelu_apprx_tanh

FEATURES, TOKENS, EXPERTS, HIDDEN, OUTPUTS = 128, 512, 2, 128, 128
PER_EXPERT = TOKENS // EXPERTS
PIECE = 128
PIECES = TOKENS // PIECE
STRIPE = 16

FLOPS = 2 * TOKENS * (FEATURES * HIDDEN + HIDDEN * OUTPUTS)


def tile_rows_ffn2_gelu_kernel(tc, table, w, b, w2, offs, out):
    nc = tc.nc
    with (
        tc.tile_pool(name="held", bufs=1) as held,
        tc.psum_pool(name="psum", bufs=1) as psum,
    ):
        offsets = held.tile([128, TOKENS // STRIPE], U16)
        tokens = held.tile([FEATURES, TOKENS], BF16)
        first_weights = held.tile([FEATURES, EXPERTS, HIDDEN], BF16)
        second_weights = held.tile([HIDDEN, EXPERTS, OUTPUTS], BF16)
        bias = held.tile([HIDDEN, EXPERTS], F32)

        nc.sync.dma_start(tokens[:], table)
        nc.sync.dma_start(offsets[:], offs)
        nc.scalar.dma_start(first_weights[:], w.rearrange("e k h -> k e h"))
        nc.scalar.dma_start(bias[:], b)
        nc.sync.dma_start(second_weights[:], w2.rearrange("e h o -> h e o"))

        warm_in = held.tile([128, 1], F32)
        warm_out = held.tile([128, 1], F32)
        nc.vector.memset(warm_in[:], 0.0)
        nc.scalar.activation(warm_out[:], warm_in[:], GELU_TANH)

        first_sums = []
        for p in range(PIECES):
            e = p * PIECE // PER_EXPERT
            first_sum = psum.tile([HIDDEN, PIECE], F32, name=f"first_sum{p}")
            columns = slice(p * PIECE // STRIPE, (p + 1) * PIECE // STRIPE)
            picked = tokens[:].indirect(offsets[:, columns])
            nc.tensor.matmul(first_sum[:], first_weights[:, e, :], picked, start=True, stop=True)
            first_sums.append(first_sum)

        for p in range(PIECES):
            e = p * PIECE // PER_EXPERT
            hidden = held.tile([HIDDEN, PIECE], BF16, name=f"hidden{p}")
            nc.scalar.activation(hidden[:], first_sums[p][:], GELU_TANH, bias=bias[:, e : e + 1])
            second_sum = psum.tile([OUTPUTS, PIECE], F32, name=f"second_sum{p}")
            nc.tensor.matmul(second_sum[:], second_weights[:, e, :], hidden[:], start=True, stop=True)
            result = held.tile([OUTPUTS, PIECE], F32, name=f"result{p}")
            nc.vector.tensor_copy(result[:], second_sum[:])
            nc.sync.dma_start(out[:, p * PIECE : (p + 1) * PIECE], result[:])
